import numpy as np
import ml_dtypes


def mxq(x, axis, fmt="e4m3"):
    dtype, down = {"e4m3": (ml_dtypes.float8_e4m3fn, 7), "e5m2": (ml_dtypes.float8_e5m2, 14)}[fmt]
    v = np.moveaxis(np.asarray(x, np.float32).astype(ml_dtypes.bfloat16).astype(np.float64), axis, -1)
    blocks = v.reshape(v.shape[:-1] + (-1, 32))
    amax = np.abs(blocks).max(-1, keepdims=True)
    byte = np.maximum(np.where(amax > 0, np.frexp(amax)[1] - 1 + 127, 0) - down, 1)
    scale = np.exp2(byte - 127.0)
    codes = (blocks / scale).astype(np.float32).astype(dtype).astype(np.float64)
    return np.moveaxis((codes * scale).reshape(v.shape), -1, axis)


WIDE = False


def mx_kscale(k):
    if not WIDE:
        return np.ones(k)
    levels = np.array([10, -10, 5, -5, 0])
    if k % 512:
        return np.exp2(np.random.permutation(np.resize(levels, k // 32))).repeat(32)
    a = np.empty((k // 512, 16))
    for p in range(k // 512):
        a[p, :8] = np.random.permutation(np.resize(levels, 8))
        for g in range(8):
            far = levels[np.abs(levels - a[p, g]) >= 10]
            a[p, g + 8] = far[np.random.randint(len(far))]
    return np.exp2(a.ravel()).repeat(32)


def f64(x):
    return np.asarray(x).astype(np.float64)


def striped(idx):
    return np.tile(idx.reshape(-1, 16).T, (8, 1)).astype(np.uint16)


def unstriped(offs):
    return offs[:16].T.reshape(-1).astype(np.int64)


def striped8(idx):
    return np.concatenate([x.reshape(-1, 16).T for x in idx]).astype(np.uint16)


def runs(offs, k):
    lists = np.stack([offs[16 * r : 16 * r + 16].T.reshape(-1) for r in range(8)]).astype(np.int64)
    return lists[np.arange(k) % 512 // 64]


def pack_weight(w):
    k, n = w.shape
    w = f64(np.asarray(w, np.float32).astype(ml_dtypes.bfloat16)).reshape(k // 32, 32, n)
    amax = np.abs(w).max(1)
    byte = np.clip(np.where(amax > 0, np.frexp(amax)[1] - 1 + 127 - 7, 1), 1, 254)
    scaled = (w * np.exp2(127.0 - byte)[:, None, :]).reshape(k, n).astype(np.float32)
    words = np.ascontiguousarray(scaled.reshape(k // 512, 128, 4, n).transpose(0, 1, 3, 2)).astype(ml_dtypes.float8_e4m3fn).view(np.uint8)
    return words, np.ascontiguousarray(byte.astype(np.uint8).reshape(k // 512, 16, n))


def unpack_weight(words, scales):
    g, p, n, _ = words.shape
    vals = np.ascontiguousarray(words).view(ml_dtypes.float8_e4m3fn).astype(np.float64) * np.repeat(np.exp2(scales.astype(np.float64) - 127.0), 8, axis=1)[..., None]
    return vals.transpose(0, 1, 3, 2).reshape(g * 512, n)


E2M1 = np.array([0.0, 0.5, 1.0, 1.5, 2.0, 3.0, 4.0, 6.0, -0.0, -0.5, -1.0, -1.5, -2.0, -3.0, -4.0, -6.0])


def pack_fp4(w):
    k, n = w.shape
    w = f64(np.asarray(w, np.float32).astype(ml_dtypes.bfloat16)).reshape(k // 32, 32, n)
    amax = np.abs(w).max(1)
    mant, ex = np.frexp(amax / 6.0)
    byte = np.clip(np.where(amax > 0, np.where(mant > 0.5, ex, ex - 1) + 127, 1), 1, 254)
    scaled = (w * np.exp2(127.0 - byte)[:, None, :]).reshape(k, n).astype(np.float32)
    c = np.ascontiguousarray(scaled.reshape(k // 512, 128, 4, n).transpose(0, 1, 3, 2)).astype(ml_dtypes.float4_e2m1fn).view(np.uint8) & 0xF
    words = (c[..., 0::2] | (c[..., 1::2] << 4)).reshape(k // 512, 128, 2 * n)
    return np.ascontiguousarray(words), np.ascontiguousarray(byte.astype(np.uint8).reshape(k // 512, 16, n))


def unpack_fp4(words, scales):
    g, _, n = scales.shape
    words = np.ascontiguousarray(words).reshape(g, 128, n, 2)
    nib = np.empty((g, 128, n, 4), np.uint8)
    nib[..., 0::2] = words & 0xF
    nib[..., 1::2] = words >> 4
    vals = E2M1[nib] * np.repeat(np.exp2(scales.astype(np.float64) - 127.0), 8, axis=1)[..., None]
    return vals.transpose(0, 1, 3, 2).reshape(g * 512, n)


K, T, S, H, G = 512, 1024, 256, 512, 2048


def setup_inputs():
    n = np.random.standard_normal
    s = mx_kscale(K)[:, None]
    packed_xT = pack_weight(n((K, T)) * s)
    packed_w1 = pack_fp4(n((K, H)) / np.sqrt(K) / s)
    packed_dT = pack_weight(n((K, G)) / s)
    return {
        "x_words": packed_xT[0],
        "x_scales": packed_xT[1],
        "w1_words": packed_w1[0],
        "w1_scales": packed_w1[1],
        "gs": (np.random.uniform(0.5, 1.5, (K, 1)) * s).astype(np.float32),
        "d_words": packed_dT[0],
        "d_scales": packed_dT[1],
        "offs": striped(np.random.permutation(T)[:S]),
        "n1": striped(np.random.permutation(S)),
        "n2": striped(np.random.permutation(S)),
        "k1": striped8(np.random.randint(0, G, (8, H))),
        "k2": striped8(np.random.randint(0, G, (8, H))),
        "hz": striped8(np.random.randint(0, T, (8, S))),
        "n3": striped(np.random.permutation(S)),
        "n4": striped(np.random.permutation(S)),
    }


def reference(x_words, x_scales, w1_words, w1_scales, gs, d_words, d_scales, offs, n1, n2, k1, k2, hz, n3, n4):
    d_k1 = unpack_weight(d_words, d_scales)[np.arange(K)[:, None], runs(k1, K)]
    xq = unpack_weight(x_words, x_scales)[:, unstriped(offs)]
    y = unpack_fp4(w1_words, w1_scales).T @ xq
    z = f64(gs) * (y[:, unstriped(n1)] - y[:, unstriped(n2)])
    d_k2 = unpack_weight(d_words, d_scales)[np.arange(K)[:, None], runs(k2, K)]
    x_hz = unpack_weight(x_words, x_scales)[np.arange(K)[:, None], runs(hz, K)]
    h = 0.0625 * ((d_k1.T @ mxq(z, 0, "e4m3") + d_k2.T @ x_hz))
    ds = np.zeros((H, S))
    ds[:, unstriped(n3)] = h
    ds2 = np.zeros((H, S))
    ds2[:, unstriped(n4)] = h
    return np.maximum(ds, ds2)

@@ -1,0 +1,234 @@
+from contextlib import ExitStack
+
+import concourse.mybir as mybir
+
+K, T, S, H, G = 512, 1024, 256, 512, 2048
+FLOPS = 3 * 2 * K * H * S
+
+F32 = mybir.dt.float32
+BF16 = mybir.dt.bfloat16
+I32 = mybir.dt.int32
+U32 = mybir.dt.uint32
+U16 = mybir.dt.uint16
+U8 = mybir.dt.uint8
+FP8X4 = mybir.dt.float8_e4m3fn_x4
+FP4X4 = mybir.dt.float4_e2m1fn_x4
+ALU = mybir.AluOpType
+COPY = mybir.ActivationFunctionType.Copy
+
+P = 128
+PACK = 4
+HALF = 128
+STRIPE = 16
+
+
+def tile_picked_cmixhgapsendtwo_none_p_kernel(
+    tc, x_words, x_scales, w1_words, w1_scales, gs, d_words, d_scales, offs, n1, n2, k1, k2, hz, n3, n4, out
+):
+    nc = tc.nc
+    with ExitStack() as ctx:
+        keep = ctx.enter_context(tc.tile_pool(name="keep", bufs=1))
+        psum = ctx.enter_context(tc.psum_pool(name="psum", bufs=1))
+
+        def sb(name, shape, dtype, slot=None):
+            return keep.tile(shape, dtype, name=name, tag=slot or name, align_bytes=64)
+
+        def load_list(name, src):
+            tile = keep.tile(list(src.shape), U16, name=name)
+            nc.sync.dma_start(tile[:], src)
+            return tile
+
+        def entries(lst, first, count):
+            return lst[:, first // STRIPE : (first + count) // STRIPE]
+
+        def zero(engine, tile):
+            engine.memset(tile[:].bitcast(I32), 0)
+
+        def load_plane_rows(queue, tile, scales, a):
+            queue.dma_start(tile[:].bitcast(I32)[a:P:32, :], scales[0].bitcast(I32)[a:16:4, :])
+
+        def load_rows(queue, tile, scales):
+            queue.dma_start(tile[:].bitcast(I32)[0:P:8, :], scales[0].bitcast(I32))
+
+        def place_rows(plane, picked):
+            for a in range(4):
+                nc.sync.dma_start(plane[:].bitcast(I32)[a:P:32, :], picked[:].bitcast(I32)[8 * a : P : 32, :])
+
+        x_plane = sb("x_plane", [P, T], U8)
+        w_plane = sb("w_plane", [P, H], U8)
+        x_rows = sb("x_rows", [P, T], U8)
+        d_rows = sb("d_rows", [P, G], U8)
+        early_plane = sb("early_plane", [P, 3 * 256], U8)
+        late_plane = sb("late_plane", [P, 2 * 256], U8)
+        zero(nc.vector, w_plane)
+        zero(nc.vector, x_plane)
+        zero(nc.vector, d_rows)
+        zero(nc.vector, x_rows)
+        zero(nc.vector, early_plane)
+        zero(nc.vector, late_plane)
+
+        x_tab = sb("x_tab", [P, T], U32)
+        d_tab = sb("d_tab", [P, G], U32)
+        w_tab = sb("w_tab", [P, 2 * H], U8)
+        gain = sb("gain", [P, PACK], F32)
+
+        nc.gpsimd.dma_start(gain[:], gs.rearrange("(p t) o -> p (t o)", t=PACK))
+        offs_sb = load_list("offs_sb", offs)
+        nc.sync.dma_start(w_tab[:].bitcast(I32), w1_words[0].bitcast(I32))
+        for a in range(4):
+            load_plane_rows(nc.sync, w_plane, w1_scales, a)
+        load_plane_rows(nc.sync, x_plane, x_scales, 0)
+        nc.sync.dma_start(x_tab[:].bitcast(I32), x_words[0].rearrange("p n t -> p (n t)").bitcast(I32))
+        load_plane_rows(nc.sync, x_plane, x_scales, 1)
+        load_plane_rows(nc.sync, x_plane, x_scales, 2)
+        load_plane_rows(nc.gpsimd, x_plane, x_scales, 3)
+        load_rows(nc.gpsimd, d_rows, d_scales)
+        load_rows(nc.gpsimd, x_rows, x_scales)
+        k2_sb = load_list("k2_sb", k2)
+        k1_sb = load_list("k1_sb", k1)
+        n1_sb = load_list("n1_sb", n1)
+        n2_sb = load_list("n2_sb", n2)
+        hz_sb = load_list("hz_sb", hz)
+        nc.sync.dma_start(d_tab[:].bitcast(I32), d_words[0].rearrange("p n t -> p (n t)").bitcast(I32))
+        n3_sb = load_list("n3_sb", n3)
+        n4_sb = load_list("n4_sb", n4)
+
+        xq_scale = sb("xq_scale", [P, S], U8)
+        xq = sb("xq", [P, S], U32)
+        nc.vector.tensor_copy(xq_scale[:], x_plane[:].indirect(offs_sb[:]))
+        nc.vector.tensor_copy(xq[:], x_tab[:].indirect(offs_sb[:]))
+        w_dealt = sb("w_dealt", [P, 2 * H], U8)
+        w_scale = sb("w_scale", [P, H], U8)
+        nc.scalar.copy(
+            w_dealt[:].bitcast(U16).rearrange("p (t m) -> p t m", t=PACK),
+            w_tab[:].bitcast(U16).rearrange("p (m t) -> p t m", t=PACK),
+        )
+        nc.vector.tensor_copy(
+            w_scale[:].rearrange("p (t m) -> p t m", t=PACK),
+            w_plane[:].rearrange("p (m t) -> p t m", t=PACK),
+        )
+        ys = []
+        for t in range(PACK):
+            acc = psum.tile([P, S], F32, name="y_acc%d" % t, tag="bank%d" % t)
+            nc.tensor.matmul_mx(
+                acc[:],
+                lhsT=w_dealt[:, 2 * P * t : 2 * P * (t + 1)].bitcast(FP4X4),
+                lhsT_scale=w_scale[:, P * t : P * (t + 1)],
+                rhs=xq[:].bitcast(FP8X4),
+                rhs_scale=xq_scale[:],
+                start=True,
+                stop=True,
+            )
+            y = sb("y%d" % t, [P, S], F32)
+            if t < 2:
+                nc.scalar.activation(y[:], acc[:], COPY, scale=gain[:, t : t + 1])
+            else:
+                nc.vector.tensor_scalar(y[:], acc[:], gain[:, t : t + 1], None, ALU.mult)
+            ys.append(y)
+
+        fetched = []
+        for c in range(2):
+            pair = sb("fetch%d" % c, [P, 2 * PACK, HALF], F32, ("fetch0", "gain")[c])
+            for t in range(PACK):
+                nc.scalar.activation(pair[:, t, :], ys[t][:].indirect(entries(n1_sb, HALF * c, HALF)), COPY)
+                nc.scalar.activation(pair[:, PACK + t, :], ys[t][:].indirect(entries(n2_sb, HALF * c, HALF)), COPY)
+            fetched.append(pair)
+
+        early_bytes = sb("early_bytes", [P, 3 * 256], U8)
+        nc.vector.tensor_copy(early_bytes[:, 0:256], d_rows[:].indirect(entries(k2_sb, 0, 256)))
+        nc.vector.tensor_copy(early_bytes[:, 256:512], d_rows[:].indirect(entries(k1_sb, 0, 256)))
+        nc.vector.tensor_copy(early_bytes[:, 512:768], x_rows[:].indirect(hz_sb[:]))
+        place_rows(early_plane, early_bytes)
+
+        x_hz = [sb("x_hz0", [P, HALF], U32)]
+        d1 = [sb("d1_0", [P, 256], U32, "d1")]
+        d2 = [sb("d2_0", [P, 256], U32, "d2")]
+        nc.vector.tensor_copy(x_hz[0][:], x_tab[:].indirect(entries(hz_sb, 0, HALF)))
+        nc.vector.tensor_copy(d2[0][:], d_tab[:].indirect(entries(k2_sb, 0, 256)))
+        nc.vector.tensor_copy(d1[0][:], d_tab[:].indirect(entries(k1_sb, 0, 256)))
+
+        zq = sb("zq", [P, S], U32)
+        z_scale = sb("z_scale", [P, S], U8)
+
+        def make_z(c):
+            pair = fetched[c]
+            z = sb("z%d" % c, [P, HALF * PACK], BF16, ("x_rows", "sixteenth")[c])
+            nc.vector.tensor_tensor(
+                z[:].rearrange("p (c i t) -> p c t i", i=4, t=PACK),
+                pair[:, 0:PACK, :].rearrange("p t (c i) -> p c t i", i=4),
+                pair[:, PACK : 2 * PACK, :].rearrange("p t (c i) -> p c t i", i=4),
+                ALU.subtract,
+            )
+            cols = slice(HALF * c, HALF * (c + 1))
+            nc.vector.quantize_mx(out=zq[:, cols].bitcast(FP8X4), scales=z_scale[:, cols], in_=z[:])
+
+        hs = [sb("h%d" % m, [P, S], F32) for m in range(4)]
+        sent3 = [sb("sent3_%d" % m, [P, S * (1 + m // 2)], F32) for m in range(4)]
+        sent4 = [sb("sent4_%d" % m, [P, S * (1 + m // 2)], F32) for m in range(4)]
+
+        sixteenth = sb("sixteenth", [P, 1], F32)
+        nc.gpsimd.memset(sixteenth[:], 0.0625)
+
+        def make_h(m, c, bank):
+            first, count = HALF * c, HALF
+            u, w = divmod(m, 2)
+            plane = (early_plane, late_plane)[u]
+            rows = slice(P * w, P * (w + 1))
+            cols = slice(first, first + count)
+            acc = psum.tile([P, count], F32, name="h_acc%d_%d" % (m, first), tag="bank%d" % bank)
+            nc.tensor.matmul_mx(
+                acc[:],
+                lhsT=d2[u][:, rows].bitcast(FP8X4),
+                lhsT_scale=plane[:, rows],
+                rhs=x_hz[c][:].bitcast(FP8X4),
+                rhs_scale=early_plane[:, 512 + first : 512 + first + count],
+                start=True,
+                stop=False,
+            )
+            nc.tensor.matmul_mx(
+                acc[:],
+                lhsT=d1[u][:, rows].bitcast(FP8X4),
+                lhsT_scale=plane[:, 256 + P * w : 256 + P * (w + 1)],
+                rhs=zq[:, cols].bitcast(FP8X4),
+                rhs_scale=z_scale[:, cols],
+                start=False,
+                stop=True,
+            )
+            nc.vector.tensor_scalar(hs[m][:, cols], acc[:], sixteenth[:] if m < 2 and c == 0 else 0.0625, None, ALU.mult)
+
+        def send(m, c):
+            cols = slice(HALF * c, HALF * (c + 1))
+            nc.scalar.activation(sent3[m][:].indirect(entries(n3_sb, HALF * c, HALF)), hs[m][:, cols], COPY)
+            nc.scalar.activation(sent4[m][:].indirect(entries(n4_sb, HALF * c, HALF)), hs[m][:, cols], COPY)
+
+        def finish(m):
+            res = sb("res%d" % m, [P, S], F32)
+            nc.vector.tensor_tensor(res[:], sent3[m][:, 0:S], sent4[m][:, 0:S], ALU.max)
+            nc.sync.dma_start(out[P * m : P * (m + 1), :], res[:])
+
+        make_z(0)
+        x_hz.append(sb("x_hz1", [P, HALF], U32, "fetch0"))
+        nc.vector.tensor_copy(x_hz[1][:], x_tab[:].indirect(entries(hz_sb, HALF, HALF)))
+        for m in range(2):
+            make_h(m, 0, 4 + m)
+            send(m, 0)
+        make_z(1)
+        for m in range(2):
+            make_h(m, 1, 6 + m)
+        late_bytes = sb("late_bytes", [P, 2 * 256], U8, "gain")
+        d1.append(sb("d1_1", [P, 256], U32, "d1"))
+        d2.append(sb("d2_1", [P, 256], U32, "d2"))
+        nc.vector.tensor_copy(late_bytes[:, 0:256], d_rows[:].indirect(entries(k2_sb, 256, 256)))
+        nc.vector.tensor_copy(late_bytes[:, 256:512], d_rows[:].indirect(entries(k1_sb, 256, 256)))
+        place_rows(late_plane, late_bytes)
+        nc.vector.tensor_copy(d2[1][:], d_tab[:].indirect(entries(k2_sb, 256, 256)))
+        nc.vector.tensor_copy(d1[1][:], d_tab[:].indirect(entries(k1_sb, 256, 256)))
+        for m in range(2):
+            send(m, 1)
+            finish(m)
+        for m in range(2, 4):
+            for c in range(2):
+                make_h(m, c, 2 * (m - 2) + c)
+            nc.scalar.activation(sent3[m][:].indirect(n3_sb[:]), hs[m][:], COPY)
+            nc.scalar.activation(sent4[m][:].indirect(n4_sb[:]), hs[m][:], COPY)
+            finish(m)

@@ -56,14 +56,12 @@ def tile_picked_cmixhgapsendtwo_none_p_kernel(
 
         x_plane = sb("x_plane", [P, T], U8)
         w_plane = sb("w_plane", [P, H], U8)
-        x_rows = sb("x_rows", [P, T], U8)
         d_rows = sb("d_rows", [P, G], U8)
         early_plane = sb("early_plane", [P, 3 * 256], U8)
         late_plane = sb("late_plane", [P, 2 * 256], U8)
-        zero(nc.vector, w_plane)
         zero(nc.vector, x_plane)
         zero(nc.vector, d_rows)
-        zero(nc.vector, x_rows)
+        zero(nc.vector, w_plane)
         zero(nc.vector, early_plane)
         zero(nc.vector, late_plane)
 
@@ -73,22 +71,20 @@ def tile_picked_cmixhgapsendtwo_none_p_kernel(
         gain = sb("gain", [P, PACK], F32)
 
         nc.gpsimd.dma_start(gain[:], gs.rearrange("(p t) o -> p (t o)", t=PACK))
+        load_rows(nc.gpsimd, d_rows, d_scales)
         offs_sb = load_list("offs_sb", offs)
+        hz_sb = load_list("hz_sb", hz)
         nc.sync.dma_start(w_tab[:].bitcast(I32), w1_words[0].bitcast(I32))
+        load_rows(nc.sync, x_plane, x_scales)
+        for a in range(1, 4):
+            load_plane_rows(nc.sync, x_plane, x_scales, a)
+        nc.sync.dma_start(x_tab[:].bitcast(I32), x_words[0].rearrange("p n t -> p (n t)").bitcast(I32))
         for a in range(4):
             load_plane_rows(nc.sync, w_plane, w1_scales, a)
-        load_plane_rows(nc.sync, x_plane, x_scales, 0)
-        nc.sync.dma_start(x_tab[:].bitcast(I32), x_words[0].rearrange("p n t -> p (n t)").bitcast(I32))
-        load_plane_rows(nc.sync, x_plane, x_scales, 1)
-        load_plane_rows(nc.sync, x_plane, x_scales, 2)
-        load_plane_rows(nc.gpsimd, x_plane, x_scales, 3)
-        load_rows(nc.gpsimd, d_rows, d_scales)
-        load_rows(nc.gpsimd, x_rows, x_scales)
         k2_sb = load_list("k2_sb", k2)
         k1_sb = load_list("k1_sb", k1)
         n1_sb = load_list("n1_sb", n1)
         n2_sb = load_list("n2_sb", n2)
-        hz_sb = load_list("hz_sb", hz)
         nc.sync.dma_start(d_tab[:].bitcast(I32), d_words[0].rearrange("p n t -> p (n t)").bitcast(I32))
         n3_sb = load_list("n3_sb", n3)
         n4_sb = load_list("n4_sb", n4)
@@ -120,7 +116,7 @@ def tile_picked_cmixhgapsendtwo_none_p_kernel(
                 stop=True,
             )
             y = sb("y%d" % t, [P, S], F32)
-            if t < 2:
+            if t == 0:
                 nc.scalar.activation(y[:], acc[:], COPY, scale=gain[:, t : t + 1])
             else:
                 nc.vector.tensor_scalar(y[:], acc[:], gain[:, t : t + 1], None, ALU.mult)
@@ -137,12 +133,12 @@ def tile_picked_cmixhgapsendtwo_none_p_kernel(
         early_bytes = sb("early_bytes", [P, 3 * 256], U8)
         nc.vector.tensor_copy(early_bytes[:, 0:256], d_rows[:].indirect(entries(k2_sb, 0, 256)))
         nc.vector.tensor_copy(early_bytes[:, 256:512], d_rows[:].indirect(entries(k1_sb, 0, 256)))
-        nc.vector.tensor_copy(early_bytes[:, 512:768], x_rows[:].indirect(hz_sb[:]))
+        nc.vector.tensor_copy(early_bytes[:, 512:768], x_plane[:].indirect(hz_sb[:]))
         place_rows(early_plane, early_bytes)
 
         x_hz = [sb("x_hz0", [P, HALF], U32)]
-        d1 = [sb("d1_0", [P, 256], U32, "d1")]
-        d2 = [sb("d2_0", [P, 256], U32, "d2")]
+        d1 = [sb("d1_0", [P, 256], U32, "w_dealt")]
+        d2 = [sb("d2_0", [P, 256], U32, "xq")]
         nc.vector.tensor_copy(x_hz[0][:], x_tab[:].indirect(entries(hz_sb, 0, HALF)))
         nc.vector.tensor_copy(d2[0][:], d_tab[:].indirect(entries(k2_sb, 0, 256)))
         nc.vector.tensor_copy(d1[0][:], d_tab[:].indirect(entries(k1_sb, 0, 256)))
@@ -152,7 +148,7 @@ def tile_picked_cmixhgapsendtwo_none_p_kernel(
 
         def make_z(c):
             pair = fetched[c]
-            z = sb("z%d" % c, [P, HALF * PACK], BF16, ("x_rows", "sixteenth")[c])
+            z = sb("z%d" % c, [P, HALF * PACK], BF16, ("early_bytes", "sixteenth")[c])
             nc.vector.tensor_tensor(
                 z[:].rearrange("p (c i t) -> p c t i", i=4, t=PACK),
                 pair[:, 0:PACK, :].rearrange("p t (c i) -> p c t i", i=4),
@@ -203,8 +199,11 @@ def tile_picked_cmixhgapsendtwo_none_p_kernel(
 
         def finish(m):
             res = sb("res%d" % m, [P, S], F32)
-            nc.vector.tensor_tensor(res[:], sent3[m][:, 0:S], sent4[m][:, 0:S], ALU.max)
-            nc.sync.dma_start(out[P * m : P * (m + 1), :], res[:])
+            parts = 2 if m == 3 else 1
+            for j in range(parts):
+                cols = slice(j * S // parts, (j + 1) * S // parts)
+                nc.vector.tensor_tensor(res[:, cols], sent3[m][:, cols], sent4[m][:, cols], ALU.max)
+                (nc.sync, nc.scalar)[j].dma_start(out[P * m : P * (m + 1), cols], res[:, cols])
 
         make_z(0)
         x_hz.append(sb("x_hz1", [P, HALF], U32, "fetch0"))
@@ -214,10 +213,10 @@ def tile_picked_cmixhgapsendtwo_none_p_kernel(
             send(m, 0)
         make_z(1)
         for m in range(2):
-            make_h(m, 1, 6 + m)
+            make_h(m, 1, 4 + m)
         late_bytes = sb("late_bytes", [P, 2 * 256], U8, "gain")
-        d1.append(sb("d1_1", [P, 256], U32, "d1"))
-        d2.append(sb("d2_1", [P, 256], U32, "d2"))
+        d1.append(sb("d1_1", [P, 256], U32, "w_dealt"))
+        d2.append(sb("d2_1", [P, 256], U32, "xq"))
         nc.vector.tensor_copy(late_bytes[:, 0:256], d_rows[:].indirect(entries(k2_sb, 256, 256)))
         nc.vector.tensor_copy(late_bytes[:, 256:512], d_rows[:].indirect(entries(k1_sb, 256, 256)))
         place_rows(late_plane, late_bytes)

from contextlib import ExitStack

import concourse.mybir as mybir

K, T, S, H, G = 512, 1024, 256, 512, 2048
FLOPS = 3 * 2 * K * H * S

F32 = mybir.dt.float32
BF16 = mybir.dt.bfloat16
I32 = mybir.dt.int32
U32 = mybir.dt.uint32
U16 = mybir.dt.uint16
U8 = mybir.dt.uint8
FP8X4 = mybir.dt.float8_e4m3fn_x4
FP4X4 = mybir.dt.float4_e2m1fn_x4
ALU = mybir.AluOpType
COPY = mybir.ActivationFunctionType.Copy

P = 128
PACK = 4
HALF = 128
STRIPE = 16


def tile_picked_cmixhgapsendtwo_none_p_kernel(
    tc, x_words, x_scales, w1_words, w1_scales, gs, d_words, d_scales, offs, n1, n2, k1, k2, hz, n3, n4, out
):
    nc = tc.nc
    with ExitStack() as ctx:
        keep = ctx.enter_context(tc.tile_pool(name="keep", bufs=1))
        psum = ctx.enter_context(tc.psum_pool(name="psum", bufs=1))

        def sb(name, shape, dtype, slot=None):
            return keep.tile(shape, dtype, name=name, tag=slot or name, align_bytes=64)

        def load_list(name, src):
            tile = keep.tile(list(src.shape), U16, name=name)
            nc.sync.dma_start(tile[:], src)
            return tile

        def entries(lst, first, count):
            return lst[:, first // STRIPE : (first + count) // STRIPE]

        def zero(engine, tile):
            engine.memset(tile[:].bitcast(I32), 0)

        def load_plane_rows(queue, tile, scales, a):
            queue.dma_start(tile[:].bitcast(I32)[a:P:32, :], scales[0].bitcast(I32)[a:16:4, :])

        def load_rows(queue, tile, scales):
            queue.dma_start(tile[:].bitcast(I32)[0:P:8, :], scales[0].bitcast(I32))

        def place_rows(plane, picked):
            for a in range(4):
                nc.sync.dma_start(plane[:].bitcast(I32)[a:P:32, :], picked[:].bitcast(I32)[8 * a : P : 32, :])

        x_plane = sb("x_plane", [P, T], U8)
        w_plane = sb("w_plane", [P, H], U8)
        d_rows = sb("d_rows", [P, G], U8)
        early_plane = sb("early_plane", [P, 3 * 256], U8)
        late_plane = sb("late_plane", [P, 2 * 256], U8)
        zero(nc.vector, x_plane)
        zero(nc.vector, d_rows)
        zero(nc.vector, w_plane)
        zero(nc.vector, early_plane)
        zero(nc.vector, late_plane)

        x_tab = sb("x_tab", [P, T], U32)
        d_tab = sb("d_tab", [P, G], U32)
        w_tab = sb("w_tab", [P, 2 * H], U8)
        gain = sb("gain", [P, PACK], F32)

        nc.gpsimd.dma_start(gain[:], gs.rearrange("(p t) o -> p (t o)", t=PACK))
        load_rows(nc.gpsimd, d_rows, d_scales)
        offs_sb = load_list("offs_sb", offs)
        hz_sb = load_list("hz_sb", hz)
        nc.sync.dma_start(w_tab[:].bitcast(I32), w1_words[0].bitcast(I32))
        load_rows(nc.sync, x_plane, x_scales)
        for a in range(1, 4):
            load_plane_rows(nc.sync, x_plane, x_scales, a)
        nc.sync.dma_start(x_tab[:].bitcast(I32), x_words[0].rearrange("p n t -> p (n t)").bitcast(I32))
        for a in range(4):
            load_plane_rows(nc.sync, w_plane, w1_scales, a)
        k2_sb = load_list("k2_sb", k2)
        k1_sb = load_list("k1_sb", k1)
        n1_sb = load_list("n1_sb", n1)
        n2_sb = load_list("n2_sb", n2)
        nc.sync.dma_start(d_tab[:].bitcast(I32), d_words[0].rearrange("p n t -> p (n t)").bitcast(I32))
        n3_sb = load_list("n3_sb", n3)
        n4_sb = load_list("n4_sb", n4)

        xq_scale = sb("xq_scale", [P, S], U8)
        xq = sb("xq", [P, S], U32)
        nc.vector.tensor_copy(xq_scale[:], x_plane[:].indirect(offs_sb[:]))
        nc.vector.tensor_copy(xq[:], x_tab[:].indirect(offs_sb[:]))
        w_dealt = sb("w_dealt", [P, 2 * H], U8)
        w_scale = sb("w_scale", [P, H], U8)
        nc.scalar.copy(
            w_dealt[:].bitcast(U16).rearrange("p (t m) -> p t m", t=PACK),
            w_tab[:].bitcast(U16).rearrange("p (m t) -> p t m", t=PACK),
        )
        nc.vector.tensor_copy(
            w_scale[:].rearrange("p (t m) -> p t m", t=PACK),
            w_plane[:].rearrange("p (m t) -> p t m", t=PACK),
        )
        ys = []
        for t in range(PACK):
            acc = psum.tile([P, S], F32, name="y_acc%d" % t, tag="bank%d" % t)
            nc.tensor.matmul_mx(
                acc[:],
                lhsT=w_dealt[:, 2 * P * t : 2 * P * (t + 1)].bitcast(FP4X4),
                lhsT_scale=w_scale[:, P * t : P * (t + 1)],
                rhs=xq[:].bitcast(FP8X4),
                rhs_scale=xq_scale[:],
                start=True,
                stop=True,
            )
            y = sb("y%d" % t, [P, S], F32)
            if t == 0:
                nc.scalar.activation(y[:], acc[:], COPY, scale=gain[:, t : t + 1])
            else:
                nc.vector.tensor_scalar(y[:], acc[:], gain[:, t : t + 1], None, ALU.mult)
            ys.append(y)

        fetched = []
        for c in range(2):
            pair = sb("fetch%d" % c, [P, 2 * PACK, HALF], F32, ("fetch0", "gain")[c])
            for t in range(PACK):
                nc.scalar.activation(pair[:, t, :], ys[t][:].indirect(entries(n1_sb, HALF * c, HALF)), COPY)
                nc.scalar.activation(pair[:, PACK + t, :], ys[t][:].indirect(entries(n2_sb, HALF * c, HALF)), COPY)
            fetched.append(pair)

        early_bytes = sb("early_bytes", [P, 3 * 256], U8)
        nc.vector.tensor_copy(early_bytes[:, 0:256], d_rows[:].indirect(entries(k2_sb, 0, 256)))
        nc.vector.tensor_copy(early_bytes[:, 256:512], d_rows[:].indirect(entries(k1_sb, 0, 256)))
        nc.vector.tensor_copy(early_bytes[:, 512:768], x_plane[:].indirect(hz_sb[:]))
        place_rows(early_plane, early_bytes)

        x_hz = [sb("x_hz0", [P, HALF], U32)]
        d1 = [sb("d1_0", [P, 256], U32, "w_dealt")]
        d2 = [sb("d2_0", [P, 256], U32, "xq")]
        nc.vector.tensor_copy(x_hz[0][:], x_tab[:].indirect(entries(hz_sb, 0, HALF)))
        nc.vector.tensor_copy(d2[0][:], d_tab[:].indirect(entries(k2_sb, 0, 256)))
        nc.vector.tensor_copy(d1[0][:], d_tab[:].indirect(entries(k1_sb, 0, 256)))

        zq = sb("zq", [P, S], U32)
        z_scale = sb("z_scale", [P, S], U8)

        def make_z(c):
            pair = fetched[c]
            z = sb("z%d" % c, [P, HALF * PACK], BF16, ("early_bytes", "sixteenth")[c])
            nc.vector.tensor_tensor(
                z[:].rearrange("p (c i t) -> p c t i", i=4, t=PACK),
                pair[:, 0:PACK, :].rearrange("p t (c i) -> p c t i", i=4),
                pair[:, PACK : 2 * PACK, :].rearrange("p t (c i) -> p c t i", i=4),
                ALU.subtract,
            )
            cols = slice(HALF * c, HALF * (c + 1))
            nc.vector.quantize_mx(out=zq[:, cols].bitcast(FP8X4), scales=z_scale[:, cols], in_=z[:])

        hs = [sb("h%d" % m, [P, S], F32) for m in range(4)]
        sent3 = [sb("sent3_%d" % m, [P, S * (1 + m // 2)], F32) for m in range(4)]
        sent4 = [sb("sent4_%d" % m, [P, S * (1 + m // 2)], F32) for m in range(4)]

        sixteenth = sb("sixteenth", [P, 1], F32)
        nc.gpsimd.memset(sixteenth[:], 0.0625)

        def make_h(m, c, bank):
            first, count = HALF * c, HALF
            u, w = divmod(m, 2)
            plane = (early_plane, late_plane)[u]
            rows = slice(P * w, P * (w + 1))
            cols = slice(first, first + count)
            acc = psum.tile([P, count], F32, name="h_acc%d_%d" % (m, first), tag="bank%d" % bank)
            nc.tensor.matmul_mx(
                acc[:],
                lhsT=d2[u][:, rows].bitcast(FP8X4),
                lhsT_scale=plane[:, rows],
                rhs=x_hz[c][:].bitcast(FP8X4),
                rhs_scale=early_plane[:, 512 + first : 512 + first + count],
                start=True,
                stop=False,
            )
            nc.tensor.matmul_mx(
                acc[:],
                lhsT=d1[u][:, rows].bitcast(FP8X4),
                lhsT_scale=plane[:, 256 + P * w : 256 + P * (w + 1)],
                rhs=zq[:, cols].bitcast(FP8X4),
                rhs_scale=z_scale[:, cols],
                start=False,
                stop=True,
            )
            nc.vector.tensor_scalar(hs[m][:, cols], acc[:], sixteenth[:] if m < 2 and c == 0 else 0.0625, None, ALU.mult)

        def send(m, c):
            cols = slice(HALF * c, HALF * (c + 1))
            nc.scalar.activation(sent3[m][:].indirect(entries(n3_sb, HALF * c, HALF)), hs[m][:, cols], COPY)
            nc.scalar.activation(sent4[m][:].indirect(entries(n4_sb, HALF * c, HALF)), hs[m][:, cols], COPY)

        def finish(m):
            res = sb("res%d" % m, [P, S], F32)
            parts = 2 if m == 3 else 1
            for j in range(parts):
                cols = slice(j * S // parts, (j + 1) * S // parts)
                nc.vector.tensor_tensor(res[:, cols], sent3[m][:, cols], sent4[m][:, cols], ALU.max)
                (nc.sync, nc.scalar)[j].dma_start(out[P * m : P * (m + 1), cols], res[:, cols])

        make_z(0)
        x_hz.append(sb("x_hz1", [P, HALF], U32, "fetch0"))
        nc.vector.tensor_copy(x_hz[1][:], x_tab[:].indirect(entries(hz_sb, HALF, HALF)))
        for m in range(2):
            make_h(m, 0, 4 + m)
            send(m, 0)
        make_z(1)
        for m in range(2):
            make_h(m, 1, 4 + m)
        late_bytes = sb("late_bytes", [P, 2 * 256], U8, "gain")
        d1.append(sb("d1_1", [P, 256], U32, "w_dealt"))
        d2.append(sb("d2_1", [P, 256], U32, "xq"))
        nc.vector.tensor_copy(late_bytes[:, 0:256], d_rows[:].indirect(entries(k2_sb, 256, 256)))
        nc.vector.tensor_copy(late_bytes[:, 256:512], d_rows[:].indirect(entries(k1_sb, 256, 256)))
        place_rows(late_plane, late_bytes)
        nc.vector.tensor_copy(d2[1][:], d_tab[:].indirect(entries(k2_sb, 256, 256)))
        nc.vector.tensor_copy(d1[1][:], d_tab[:].indirect(entries(k1_sb, 256, 256)))
        for m in range(2):
            send(m, 1)
            finish(m)
        for m in range(2, 4):
            for c in range(2):
                make_h(m, c, 2 * (m - 2) + c)
            nc.scalar.activation(sent3[m][:].indirect(n3_sb[:]), hs[m][:], COPY)
            nc.scalar.activation(sent4[m][:].indirect(n4_sb[:]), hs[m][:], COPY)
            finish(m)
